import numpy as np
import ml_dtypes


def mxq(x, axis, fmt="e4m3"):
    dtype, down = {"e4m3": (ml_dtypes.float8_e4m3fn, 7), "e5m2": (ml_dtypes.float8_e5m2, 14)}[fmt]
    v = np.moveaxis(np.asarray(x, np.float32).astype(ml_dtypes.bfloat16).astype(np.float64), axis, -1)
    blocks = v.reshape(v.shape[:-1] + (-1, 32))
    amax = np.abs(blocks).max(-1, keepdims=True)
    byte = np.maximum(np.where(amax > 0, np.frexp(amax)[1] - 1 + 127, 0) - down, 1)
    scale = np.exp2(byte - 127.0)
    codes = (blocks / scale).astype(np.float32).astype(dtype).astype(np.float64)
    return np.moveaxis((codes * scale).reshape(v.shape), -1, axis)


WIDE = False


def mx_kscale(k):
    if not WIDE:
        return np.ones(k)
    levels = np.array([10, -10, 5, -5, 0])
    if k % 512:
        return np.exp2(np.random.permutation(np.resize(levels, k // 32))).repeat(32)
    a = np.empty((k // 512, 16))
    for p in range(k // 512):
        a[p, :8] = np.random.permutation(np.resize(levels, 8))
        for g in range(8):
            far = levels[np.abs(levels - a[p, g]) >= 10]
            a[p, g + 8] = far[np.random.randint(len(far))]
    return np.exp2(a.ravel()).repeat(32)


def f64(x):
    return np.asarray(x).astype(np.float64)


def striped8(idx):
    return np.asarray(idx).reshape(8, -1, 16).transpose(0, 2, 1).reshape(128, -1).astype(np.uint16)


def unstriped8(offs):
    return offs.reshape(8, 16, -1).transpose(0, 2, 1).reshape(8, -1).astype(np.int64)


def pick8(x, idx, run):
    r = np.arange(len(x))
    return x[r[:, None], idx[r % (8 * run) // run]]


E2M1 = np.array([0.0, 0.5, 1.0, 1.5, 2.0, 3.0, 4.0, 6.0, -0.0, -0.5, -1.0, -1.5, -2.0, -3.0, -4.0, -6.0])


def pack_weight(w, fmt):
    k, n = w.shape
    w = f64(np.asarray(w, np.float32).astype(ml_dtypes.bfloat16)).reshape(k // 32, 32, n)
    amax = np.abs(w).max(1)
    if fmt == "e4m3":
        byte = np.frexp(amax)[1] - 1 + 127 - 7
    else:
        mant, ex = np.frexp(amax / 6.0)
        byte = np.where(mant > 0.5, ex, ex - 1) + 127
    byte = np.clip(np.where(amax > 0, byte, 1), 1, 254)
    scaled = (w * np.exp2(127.0 - byte)[:, None, :]).reshape(k, n).astype(np.float32)
    by_word = np.ascontiguousarray(scaled.reshape(k // 512, 128, 4, n).transpose(0, 1, 3, 2))
    if fmt == "e4m3":
        words = by_word.astype(ml_dtypes.float8_e4m3fn).view(np.uint8)
    else:
        c = by_word.astype(ml_dtypes.float4_e2m1fn).view(np.uint8) & 0xF
        words = (c[..., 0::2] | (c[..., 1::2] << 4)).reshape(k // 512, 128, 2 * n)
    return np.ascontiguousarray(words), np.ascontiguousarray(byte.astype(np.uint8).reshape(k // 512, 16, n))


def unpack_weight(words, scales, fmt):
    g, _, n = scales.shape
    words = np.ascontiguousarray(words).reshape(g, 128, n, -1)
    if fmt == "e4m3":
        vals = words.view(ml_dtypes.float8_e4m3fn).astype(np.float64)
    else:
        nib = np.empty((g, 128, n, 4), np.uint8)
        nib[..., 0::2] = words & 0xF
        nib[..., 1::2] = words >> 4
        vals = E2M1[nib]
    vals = vals * np.repeat(np.exp2(scales.astype(np.float64) - 127.0), 8, axis=1)[..., None]
    return vals.transpose(0, 1, 3, 2).reshape(g * 512, n)


def softplus(v):
    return np.log(1.0 + np.exp(v))


D, T, I, Q, G = 512, 1024, 512, 128, 64


def setup_inputs():
    n = np.random.standard_normal
    idx = np.stack([np.random.permutation(T)[:I] for _ in range(8)])
    idx2 = np.stack([np.random.permutation(T)[:I] for _ in range(8)])
    fd = mx_kscale(D)
    keysp = pack_weight(n((D, T)) / fd[:, None], "e4m3")
    return {
        "query": (n((D, Q)) * 0.9 / np.sqrt(D) * fd[:, None]).astype(np.float32),
        "query2": (n((D, Q)) * 0.9 / np.sqrt(D) * fd[:, None]).astype(np.float32),
        "keys_words": keysp[0],
        "keys_scales": keysp[1],
        "lam": (np.random.uniform(0.6, 1.2, (Q, 1))).astype(np.float32),
        "mix": (np.random.uniform(0.2, 0.8, (Q, 1))).astype(np.float32),
        "old": (np.random.uniform(0.0, 2.0, (Q, T))).astype(np.float32),
        "fade": (np.random.uniform(0.3, 0.9, (Q, 1))).astype(np.float32),
        "offs": striped8(idx),
        "offs2": striped8(idx2),
    }


def reference(query, query2, keys_words, keys_scales, lam, mix, old, fade, offs, offs2):
    idx = unstriped8(offs)
    idx2 = unstriped8(offs2)
    keysu = unpack_weight(keys_words, keys_scales, "e4m3")
    queryq = mxq(f64(query), 0, "e4m3")
    a = queryq.T @ keysu
    query2q = mxq(f64(query2), 0, "e4m3")
    b = query2q.T @ keysu
    s = pick8(a, idx, 16) / (softplus(pick8(b, idx2, 16)) + 0.5) * f64(lam)
    p = np.exp(s - np.max(s, axis=1, keepdims=True))
    r = p / np.sum(p, axis=1, keepdims=True)
    pm = r.reshape(Q, G, I // G).mean(axis=2)
    pr = np.repeat(pm, I // G, axis=1)
    w = r * (1.0 - f64(mix)) + pr * f64(mix)
    ws = w * 256.0
    wf = np.zeros((Q, T))
    wf[np.arange(Q)[:, None], idx[np.arange(Q) % 128 // 16]] = ws
    y = f64(old) * f64(fade) + wf
    return y

@@ -1,0 +1,188 @@
+from contextlib import ExitStack
+
+import concourse.mybir as mybir
+
+D, T, SLOTS, Q, RUN = 512, 1024, 512, 128, 8
+FLOPS = 2 * 2 * D * Q * T
+
+F32 = mybir.dt.float32
+BF16 = mybir.dt.bfloat16
+I32 = mybir.dt.int32
+U32 = mybir.dt.uint32
+U16 = mybir.dt.uint16
+U8 = mybir.dt.uint8
+FP8X4 = mybir.dt.float8_e4m3fn_x4
+ALU = mybir.AluOpType
+ACT = mybir.ActivationFunctionType
+AX = mybir.AxisListType
+
+P = 128
+PACK = 4
+KEY_HALF = T // 2
+N_MM = 256
+HALF = SLOTS // 2
+OFF_COLS = HALF // 16
+EXP_CAP = 2.0 ** 60
+N_STORE = 256
+
+
+def quantize_queries(nc, pool, raw, tag):
+    grouped = pool.tile([P, Q, PACK], BF16, name=tag + "_grouped", align_bytes=64)
+    codes = pool.tile([P, Q], U32, name=tag + "_codes", align_bytes=64)
+    scales = pool.tile([P, Q], U8, name=tag + "_scales", align_bytes=64)
+    nc.vector.tensor_copy(
+        out=grouped[:].rearrange("p (c i) t -> p c t i", i=4),
+        in_=raw[:].rearrange("p t (c i) -> p c t i", i=4),
+    )
+    nc.vector.quantize_mx(
+        out=codes[:].bitcast(FP8X4), scales=scales[:], in_=grouped[:].rearrange("p w t -> p (w t)")
+    )
+    return codes, scales
+
+
+def tile_attend_worthfor_smoothpage_counts_heads_kernel(
+    tc, query, query2, keys_words, keys_scales, lam, mix, old, fade, offs, offs2, out
+):
+    nc = tc.nc
+    with ExitStack() as ctx:
+        sb = ctx.enter_context(tc.tile_pool(name="sb", bufs=1))
+        psum = ctx.enter_context(tc.psum_pool(name="psum", bufs=1))
+
+        offs_sb = sb.tile([P, SLOTS // 16], U16, name="offs_sb")
+        offs2_sb = sb.tile([P, SLOTS // 16], U16, name="offs2_sb")
+        key_scales = sb.tile([P, KEY_HALF], U8, name="key_scales", align_bytes=64)
+        nc.vector.memset(key_scales[:].bitcast(I32), 0)
+
+        q2_raw = sb.tile([P, PACK, Q], F32, name="q2_raw")
+        nc.sync.dma_start(out=q2_raw[:], in_=query2.rearrange("(p t) w -> p t w", t=PACK))
+        words = keys_words[0].rearrange("p n t -> p (n t)").bitcast(I32)
+        key_codes = [sb.tile([P, KEY_HALF], U32, name=f"key_codes{h}", align_bytes=64) for h in range(2)]
+        nc.sync.dma_start(out=key_codes[0][:].bitcast(I32), in_=words[:, 0:KEY_HALF])
+        scale_words = keys_scales[0].bitcast(I32)
+        for quad in range(4):
+            nc.sync.dma_start(
+                out=key_scales[32 * quad : 32 * quad + 8, :].bitcast(I32),
+                in_=scale_words[4 * quad : 4 * quad + 4, :].rearrange("r (h c) -> h r c", h=2),
+            )
+        nc.sync.dma_start(out=key_codes[1][:].bitcast(I32), in_=words[:, KEY_HALF:T])
+        nc.sync.dma_start(offs2_sb[:], offs2)
+        q_raw = sb.tile([P, PACK, Q], F32, name="q_raw")
+        nc.sync.dma_start(out=q_raw[:], in_=query.rearrange("(p t) w -> p t w", t=PACK))
+        nc.sync.dma_start(offs_sb[:], offs)
+        old_sb = sb.tile([P, T], F32, name="old_sb")
+        nc.sync.dma_start(out=old_sb[:], in_=old)
+        lam_sb = sb.tile([P, 1], F32, name="lam_sb")
+        mix_sb = sb.tile([P, 1], F32, name="mix_sb")
+        fade_sb = sb.tile([P, 1], F32, name="fade_sb")
+        nc.gpsimd.dma_start(out=lam_sb[:], in_=lam)
+        nc.gpsimd.dma_start(out=mix_sb[:], in_=mix)
+        nc.gpsimd.dma_start(out=fade_sb[:], in_=fade)
+
+        one = sb.tile([P, 1], F32, name="one")
+        half = sb.tile([P, 1], F32, name="half")
+        wf = sb.tile([P, T], F32, name="wf")
+        nc.vector.memset(one[:], 1.0)
+        nc.vector.memset(half[:], 0.5)
+        nc.vector.memset(wf[:], 0.0)
+        own_coef = sb.tile([P, 1], F32, name="own_coef")
+        run_coef = sb.tile([P, 1], F32, name="run_coef")
+        nc.gpsimd.tensor_scalar(own_coef[:], mix_sb[:], -256.0, 256.0, ALU.mult, ALU.add)
+        nc.gpsimd.tensor_scalar(run_coef[:], mix_sb[:], 256.0 / RUN, 0.0, ALU.mult, ALU.add)
+
+        def scores(codes, scales, tag, engines):
+            whole = sb.tile([P, T], F32, name=tag)
+            for n in range(T // N_MM):
+                h, c0 = divmod(n * N_MM, KEY_HALF)
+                acc = psum.tile([P, N_MM], F32, name=f"{tag}_acc{n}")
+                nc.tensor.matmul_mx(
+                    out=acc[:],
+                    lhsT=codes[:].bitcast(FP8X4),
+                    lhsT_scale=scales[:],
+                    rhs=key_codes[h][:, c0 : c0 + N_MM].bitcast(FP8X4),
+                    rhs_scale=key_scales[4 * h : P, c0 : c0 + N_MM],
+                    start=True,
+                    stop=True,
+                )
+                dst = whole[:, n * N_MM : (n + 1) * N_MM]
+                if engines[n % len(engines)] == "scalar":
+                    nc.scalar.activation(dst, acc[:], ACT.Copy)
+                else:
+                    nc.vector.tensor_copy(dst, acc[:])
+            return whole
+
+        halves = [slice(h * HALF, (h + 1) * HALF) for h in range(2)]
+        off_halves = [slice(h * OFF_COLS, (h + 1) * OFF_COLS) for h in range(2)]
+
+        q2_codes, q2_scales = quantize_queries(nc, sb, q2_raw, "q2")
+        b_all = scores(q2_codes, q2_scales, "b_all", ("scalar", "vector"))
+
+        b_sel = sb.tile([P, SLOTS], F32, name="b_sel")
+        e = sb.tile([P, SLOTS], F32, name="e")
+        e_cap = sb.tile([P, SLOTS], F32, name="e_cap")
+        for h in range(2):
+            nc.vector.tensor_copy(b_sel[:, halves[h]], b_all[:].indirect(offs2_sb[:, off_halves[h]]))
+            nc.scalar.activation(e[:, halves[h]], b_sel[:, halves[h]], ACT.Exp)
+        for h in range(2):
+            nc.vector.tensor_scalar(e_cap[:, halves[h]], e[:, halves[h]], EXP_CAP, None, ALU.min)
+
+        q_codes, q_scales = quantize_queries(nc, sb, q_raw, "q")
+        a_all = scores(q_codes, q_scales, "a_all", ("vector",))
+
+        log1p = sb.tile([P, SLOTS], F32, name="log1p")
+        soft = sb.tile([P, SLOTS], F32, name="soft")
+        log_den = sb.tile([P, SLOTS], F32, name="log_den")
+        inv_den = sb.tile([P, SLOTS], F32, name="inv_den")
+        for h in range(2):
+            nc.scalar.activation(log1p[:, halves[h]], e_cap[:, halves[h]], ACT.Ln, bias=one[:])
+            nc.vector.tensor_tensor(soft[:, halves[h]], log1p[:, halves[h]], b_sel[:, halves[h]], ALU.max)
+        for h in range(2):
+            nc.scalar.activation(log_den[:, halves[h]], soft[:, halves[h]], ACT.Ln, bias=half[:])
+        a_sel = sb.tile([P, SLOTS], F32, name="a_sel")
+        nc.vector.tensor_copy(a_sel[:], a_all[:].indirect(offs_sb[:]))
+        s = sb.tile([P, SLOTS], F32, name="s")
+        for h in range(2):
+            nc.scalar.activation(inv_den[:, halves[h]], log_den[:, halves[h]], ACT.Exp, scale=-1.0)
+            nc.vector.scalar_tensor_tensor(
+                s[:, halves[h]], a_sel[:, halves[h]], lam_sb[:], inv_den[:, halves[h]], ALU.mult, ALU.mult
+            )
+        neg_max = sb.tile([P, 1], F32, name="neg_max")
+        nc.vector.tensor_reduce(neg_max[:], s[:], AX.X, ALU.max, negate=True)
+
+        p = sb.tile([P, SLOTS], F32, name="p")
+        part_sum = sb.tile([P, 2], F32, name="part_sum")
+        run_sum = sb.tile([P, SLOTS // RUN], F32, name="run_sum")
+        runs = HALF // RUN
+        for h in range(2):
+            nc.scalar.activation(
+                p[:, halves[h]], s[:, halves[h]], ACT.Exp, bias=neg_max[:], accum_out=part_sum[:, h : h + 1]
+            )
+            nc.vector.tensor_reduce(
+                run_sum[:, h * runs : (h + 1) * runs],
+                p[:, halves[h]].rearrange("p (g r) -> p g r", r=RUN),
+                AX.X,
+                ALU.add,
+            )
+        total = sb.tile([P, 1], F32, name="total")
+        inv_total = sb.tile([P, 1], F32, name="inv_total")
+        own_w = sb.tile([P, 1], F32, name="own_w")
+        run_w = sb.tile([P, SLOTS // RUN], F32, name="run_w")
+        nc.vector.tensor_tensor(total[:], part_sum[:, 0:1], part_sum[:, 1:2], ALU.add)
+        nc.vector.reciprocal(inv_total[:], total[:])
+        nc.vector.tensor_tensor(own_w[:], own_coef[:], inv_total[:], ALU.mult)
+        nc.vector.tensor_scalar(run_w[:], run_sum[:], run_coef[:], inv_total[:], ALU.mult, ALU.mult)
+        ws = sb.tile([P, SLOTS], F32, name="ws")
+        nc.vector.scalar_tensor_tensor(
+            ws[:].rearrange("p (g r) -> p g r", r=RUN),
+            p[:].rearrange("p (g r) -> p g r", r=RUN),
+            own_w[:],
+            run_w[:].unsqueeze(2).to_broadcast([P, SLOTS // RUN, RUN]),
+            ALU.mult,
+            ALU.add,
+        )
+        nc.vector.tensor_copy(wf[:].indirect(offs_sb[:]), ws[:])
+
+        for c0 in range(0, T, N_STORE):
+            cols = slice(c0, c0 + N_STORE)
+            y = sb.tile([P, N_STORE], F32, name=f"y{c0}")
+            nc.vector.scalar_tensor_tensor(y[:], old_sb[:, cols], fade_sb[:], wf[:, cols], ALU.mult, ALU.add)
+            nc.sync.dma_start(out=out[:, cols], in_=y[:])

@@ -1,3 +1,4 @@
+import math
 from contextlib import ExitStack
 
 import concourse.mybir as mybir
@@ -18,12 +19,17 @@ AX = mybir.AxisListType
 
 P = 128
 PACK = 4
-KEY_HALF = T // 2
 N_MM = 256
 HALF = SLOTS // 2
-OFF_COLS = HALF // 16
 EXP_CAP = 2.0 ** 60
-N_STORE = 256
+SQRT_E = math.sqrt(math.e)
+N_DIVIDE = 96
+N_FIRST = 160
+STORE_WIDTHS = (256,256,256,256)
+
+
+def offsets(tile, slots):
+    return tile[:, slots.start // 16 : slots.stop // 16]
 
 
 def quantize_queries(nc, pool, raw, tag):
@@ -50,139 +56,162 @@ def tile_attend_worthfor_smoothpage_counts_heads_kernel(
 
         offs_sb = sb.tile([P, SLOTS // 16], U16, name="offs_sb")
         offs2_sb = sb.tile([P, SLOTS // 16], U16, name="offs2_sb")
-        key_scales = sb.tile([P, KEY_HALF], U8, name="key_scales", align_bytes=64)
+        key_scales = sb.tile([P, T], U8, name="key_scales", align_bytes=64)
         nc.vector.memset(key_scales[:].bitcast(I32), 0)
+        scale_words = keys_scales[0].bitcast(I32)
+        for quad in range(4):
+            nc.scalar.dma_start(
+                out=key_scales[32 * quad : 32 * quad + 4, :].bitcast(I32),
+                in_=scale_words[4 * quad : 4 * quad + 4, :],
+            )
 
         q2_raw = sb.tile([P, PACK, Q], F32, name="q2_raw")
         nc.sync.dma_start(out=q2_raw[:], in_=query2.rearrange("(p t) w -> p t w", t=PACK))
         words = keys_words[0].rearrange("p n t -> p (n t)").bitcast(I32)
-        key_codes = [sb.tile([P, KEY_HALF], U32, name=f"key_codes{h}", align_bytes=64) for h in range(2)]
-        nc.sync.dma_start(out=key_codes[0][:].bitcast(I32), in_=words[:, 0:KEY_HALF])
-        scale_words = keys_scales[0].bitcast(I32)
-        for quad in range(4):
-            nc.sync.dma_start(
-                out=key_scales[32 * quad : 32 * quad + 8, :].bitcast(I32),
-                in_=scale_words[4 * quad : 4 * quad + 4, :].rearrange("r (h c) -> h r c", h=2),
-            )
-        nc.sync.dma_start(out=key_codes[1][:].bitcast(I32), in_=words[:, KEY_HALF:T])
-        nc.sync.dma_start(offs2_sb[:], offs2)
+        key_codes = [sb.tile([P, T // 2], U32, name=f"key_codes{h}", align_bytes=64) for h in range(2)]
+        for h in range(2):
+            nc.sync.dma_start(out=key_codes[h][:].bitcast(I32), in_=words[:, h * T // 2 : (h + 1) * T // 2])
         q_raw = sb.tile([P, PACK, Q], F32, name="q_raw")
         nc.sync.dma_start(out=q_raw[:], in_=query.rearrange("(p t) w -> p t w", t=PACK))
+        nc.sync.dma_start(offs2_sb[:], offs2)
         nc.sync.dma_start(offs_sb[:], offs)
-        old_sb = sb.tile([P, T], F32, name="old_sb")
-        nc.sync.dma_start(out=old_sb[:], in_=old)
         lam_sb = sb.tile([P, 1], F32, name="lam_sb")
         mix_sb = sb.tile([P, 1], F32, name="mix_sb")
         fade_sb = sb.tile([P, 1], F32, name="fade_sb")
-        nc.gpsimd.dma_start(out=lam_sb[:], in_=lam)
-        nc.gpsimd.dma_start(out=mix_sb[:], in_=mix)
-        nc.gpsimd.dma_start(out=fade_sb[:], in_=fade)
+        old_sb = sb.tile([P, T], F32, name="old_sb")
+        nc.sync.dma_start(out=lam_sb[:], in_=lam)
+        nc.sync.dma_start(out=mix_sb[:], in_=mix)
+        nc.sync.dma_start(out=fade_sb[:], in_=fade)
+        nc.sync.dma_start(out=old_sb[:], in_=old)
 
         one = sb.tile([P, 1], F32, name="one")
-        half = sb.tile([P, 1], F32, name="half")
+        sqrt_e = sb.tile([P, 1], F32, name="sqrt_e")
         wf = sb.tile([P, T], F32, name="wf")
         nc.vector.memset(one[:], 1.0)
-        nc.vector.memset(half[:], 0.5)
+        nc.scalar.activation(sqrt_e[:], one[:], ACT.Copy, scale=SQRT_E)
         nc.vector.memset(wf[:], 0.0)
-        own_coef = sb.tile([P, 1], F32, name="own_coef")
-        run_coef = sb.tile([P, 1], F32, name="run_coef")
-        nc.gpsimd.tensor_scalar(own_coef[:], mix_sb[:], -256.0, 256.0, ALU.mult, ALU.add)
-        nc.gpsimd.tensor_scalar(run_coef[:], mix_sb[:], 256.0 / RUN, 0.0, ALU.mult, ALU.add)
+        coef = sb.tile([P, 2], F32, name="coef")
+        nc.gpsimd.tensor_scalar(coef[:, 0:1], mix_sb[:], -256.0, 256.0, ALU.mult, ALU.add)
+        nc.gpsimd.tensor_scalar(coef[:, 1:2], mix_sb[:], 256.0 / RUN, 0.0, ALU.mult, ALU.add)
 
-        def scores(codes, scales, tag, engines):
+        def scores(codes, scales, tag, widths, on_scalar):
             whole = sb.tile([P, T], F32, name=tag)
-            for n in range(T // N_MM):
-                h, c0 = divmod(n * N_MM, KEY_HALF)
-                acc = psum.tile([P, N_MM], F32, name=f"{tag}_acc{n}")
+            c0 = 0
+            for n, width in enumerate(widths):
+                cols = slice(c0, c0 + width)
+                h, k0 = divmod(c0, T // 2)
+                acc = psum.tile([P, width], F32, name=f"{tag}_acc{n}")
                 nc.tensor.matmul_mx(
                     out=acc[:],
                     lhsT=codes[:].bitcast(FP8X4),
                     lhsT_scale=scales[:],
-                    rhs=key_codes[h][:, c0 : c0 + N_MM].bitcast(FP8X4),
-                    rhs_scale=key_scales[4 * h : P, c0 : c0 + N_MM],
+                    rhs=key_codes[h][:, k0 : k0 + width].bitcast(FP8X4),
+                    rhs_scale=key_scales[:, cols],
                     start=True,
                     stop=True,
                 )
-                dst = whole[:, n * N_MM : (n + 1) * N_MM]
-                if engines[n % len(engines)] == "scalar":
-                    nc.scalar.activation(dst, acc[:], ACT.Copy)
+                if n < on_scalar:
+                    nc.scalar.activation(whole[:, cols], acc[:], ACT.Copy)
                 else:
-                    nc.vector.tensor_copy(dst, acc[:])
+                    nc.vector.tensor_copy(whole[:, cols], acc[:])
+                c0 += width
             return whole
 
-        halves = [slice(h * HALF, (h + 1) * HALF) for h in range(2)]
-        off_halves = [slice(h * OFF_COLS, (h + 1) * OFF_COLS) for h in range(2)]
+        low, high = slice(0, HALF), slice(HALF, SLOTS)
 
         q2_codes, q2_scales = quantize_queries(nc, sb, q2_raw, "q2")
-        b_all = scores(q2_codes, q2_scales, "b_all", ("scalar", "vector"))
+        q_codes, q_scales = quantize_queries(nc, sb, q_raw, "q")
+        b_all = scores(q2_codes, q2_scales, "b_all", (256, 256, 256, 128, 128), 3)
 
         b_sel = sb.tile([P, SLOTS], F32, name="b_sel")
         e = sb.tile([P, SLOTS], F32, name="e")
         e_cap = sb.tile([P, SLOTS], F32, name="e_cap")
-        for h in range(2):
-            nc.vector.tensor_copy(b_sel[:, halves[h]], b_all[:].indirect(offs2_sb[:, off_halves[h]]))
-            nc.scalar.activation(e[:, halves[h]], b_sel[:, halves[h]], ACT.Exp)
-        for h in range(2):
-            nc.vector.tensor_scalar(e_cap[:, halves[h]], e[:, halves[h]], EXP_CAP, None, ALU.min)
+        nc.scalar.activation(e[:, high], b_all[:].indirect(offsets(offs2_sb, high)), ACT.Exp)
+        nc.vector.tensor_copy(b_sel[:, low], b_all[:].indirect(offsets(offs2_sb, low)))
+        nc.scalar.activation(e[:, low], b_sel[:, low], ACT.Exp)
 
-        q_codes, q_scales = quantize_queries(nc, sb, q_raw, "q")
-        a_all = scores(q_codes, q_scales, "a_all", ("vector",))
+        nc.vector.tensor_copy(b_sel[:, high], b_all[:].indirect(offsets(offs2_sb, high)))
+        nc.vector.tensor_scalar(e_cap[:], e[:], EXP_CAP, None, ALU.min)
 
-        log1p = sb.tile([P, SLOTS], F32, name="log1p")
-        soft = sb.tile([P, SLOTS], F32, name="soft")
+        a_all = scores(q_codes, q_scales, "a_all", (512, 512), 0)
+        a_sel = sb.tile([P, SLOTS], F32, name="a_sel")
+        nc.vector.tensor_copy(a_sel[:, high], a_all[:].indirect(offsets(offs_sb, high)))
+
+        n_logged = SLOTS - N_DIVIDE
+        divided = slice(n_logged, SLOTS)
+        logged = [slice(n_logged * k // 3, n_logged * (k + 1) // 3) for k in range(3)]
+        capped_den = sb.tile([P, SLOTS], F32, name="capped_den")
+        den = sb.tile([P, SLOTS], F32, name="den")
         log_den = sb.tile([P, SLOTS], F32, name="log_den")
         inv_den = sb.tile([P, SLOTS], F32, name="inv_den")
-        for h in range(2):
-            nc.scalar.activation(log1p[:, halves[h]], e_cap[:, halves[h]], ACT.Ln, bias=one[:])
-            nc.vector.tensor_tensor(soft[:, halves[h]], log1p[:, halves[h]], b_sel[:, halves[h]], ALU.max)
-        for h in range(2):
-            nc.scalar.activation(log_den[:, halves[h]], soft[:, halves[h]], ACT.Ln, bias=half[:])
-        a_sel = sb.tile([P, SLOTS], F32, name="a_sel")
-        nc.vector.tensor_copy(a_sel[:], a_all[:].indirect(offs_sb[:]))
-        s = sb.tile([P, SLOTS], F32, name="s")
-        for h in range(2):
-            nc.scalar.activation(inv_den[:, halves[h]], log_den[:, halves[h]], ACT.Exp, scale=-1.0)
-            nc.vector.scalar_tensor_tensor(
-                s[:, halves[h]], a_sel[:, halves[h]], lam_sb[:], inv_den[:, halves[h]], ALU.mult, ALU.mult
-            )
-        neg_max = sb.tile([P, 1], F32, name="neg_max")
-        nc.vector.tensor_reduce(neg_max[:], s[:], AX.X, ALU.max, negate=True)
+        for part in logged + [divided]:
+            nc.scalar.activation(capped_den[:, part], e_cap[:, part], ACT.Ln, bias=sqrt_e[:], scale=SQRT_E)
+            nc.vector.scalar_tensor_tensor(den[:, part], b_sel[:, part], 0.5, capped_den[:, part], ALU.add, ALU.max)
+        for part in logged:
+            nc.scalar.activation(log_den[:, part], den[:, part], ACT.Ln)
 
+        nc.vector.tensor_copy(a_sel[:, low], a_all[:].indirect(offsets(offs_sb, low)))
+        nc.vector.reciprocal(inv_den[:, divided], den[:, divided])
+        s_tile = sb.tile([P, 1 + SLOTS], F32, name="s_tile")
+        s = s_tile[:, 1:]
+
+        def slot_scores(part):
+            nc.vector.scalar_tensor_tensor(s[:, part], a_sel[:, part], lam_sb[:], inv_den[:, part], ALU.mult, ALU.mult)
+
+        slot_scores(divided)
+        nc.vector.tensor_reduce(s_tile[:, 0:1], s[:, divided], AX.X, ALU.max)
+        for part in (low, slice(HALF, n_logged)):
+            nc.scalar.activation(inv_den[:, part], log_den[:, part], ACT.Exp, scale=-1.0)
+            slot_scores(part)
+        neg_max = sb.tile([P, 1], F32, name="neg_max")
+        nc.vector.tensor_reduce(neg_max[:], s_tile[:, 0 : 1 + n_logged], AX.X, ALU.max, negate=True)
+
+        first, rest = slice(0, N_FIRST), slice(N_FIRST, SLOTS)
+        n_rest = SLOTS - N_FIRST
         p = sb.tile([P, SLOTS], F32, name="p")
         part_sum = sb.tile([P, 2], F32, name="part_sum")
-        run_sum = sb.tile([P, SLOTS // RUN], F32, name="run_sum")
-        runs = HALF // RUN
-        for h in range(2):
+        run_sum_first = sb.tile([P, N_FIRST // RUN], F32, name="run_sum_first")
+        run_sum_rest = sb.tile([P, n_rest // RUN], F32, name="run_sum_rest")
+        for k, part in enumerate((first, rest)):
             nc.scalar.activation(
-                p[:, halves[h]], s[:, halves[h]], ACT.Exp, bias=neg_max[:], accum_out=part_sum[:, h : h + 1]
+                p[:, part], s[:, part], ACT.Exp, bias=neg_max[:], accum_out=part_sum[:, k : k + 1]
             )
-            nc.vector.tensor_reduce(
-                run_sum[:, h * runs : (h + 1) * runs],
-                p[:, halves[h]].rearrange("p (g r) -> p g r", r=RUN),
-                AX.X,
-                ALU.add,
-            )
+
+        def by_runs(ap):
+            return ap.rearrange("p (g r) -> p g r", r=RUN)
+
+        def spread(ap, n):
+            return ap.unsqueeze(2).to_broadcast([P, n // RUN, RUN])
+
+        run_part = sb.tile([P, N_FIRST // RUN], F32, name="run_part")
+        mixed = sb.tile([P, N_FIRST], F32, name="mixed")
+        nc.vector.tensor_reduce(run_sum_first[:], by_runs(p[:, first]), AX.X, ALU.add)
+        nc.vector.tensor_scalar(run_part[:], run_sum_first[:], coef[:, 1:2], None, ALU.mult)
+        nc.vector.scalar_tensor_tensor(
+            by_runs(mixed[:]), by_runs(p[:, first]), coef[:, 0:1], spread(run_part[:], N_FIRST), ALU.mult, ALU.add
+        )
         total = sb.tile([P, 1], F32, name="total")
         inv_total = sb.tile([P, 1], F32, name="inv_total")
-        own_w = sb.tile([P, 1], F32, name="own_w")
-        run_w = sb.tile([P, SLOTS // RUN], F32, name="run_w")
+        weight = sb.tile([P, 2], F32, name="weight")
+        ws_first = sb.tile([P, N_FIRST], F32, name="ws_first")
         nc.vector.tensor_tensor(total[:], part_sum[:, 0:1], part_sum[:, 1:2], ALU.add)
+        nc.vector.tensor_reduce(run_sum_rest[:], by_runs(p[:, rest]), AX.X, ALU.add)
         nc.vector.reciprocal(inv_total[:], total[:])
-        nc.vector.tensor_tensor(own_w[:], own_coef[:], inv_total[:], ALU.mult)
-        nc.vector.tensor_scalar(run_w[:], run_sum[:], run_coef[:], inv_total[:], ALU.mult, ALU.mult)
-        ws = sb.tile([P, SLOTS], F32, name="ws")
-        nc.vector.scalar_tensor_tensor(
-            ws[:].rearrange("p (g r) -> p g r", r=RUN),
-            p[:].rearrange("p (g r) -> p g r", r=RUN),
-            own_w[:],
-            run_w[:].unsqueeze(2).to_broadcast([P, SLOTS // RUN, RUN]),
-            ALU.mult,
-            ALU.add,
-        )
-        nc.vector.tensor_copy(wf[:].indirect(offs_sb[:]), ws[:])
+        nc.vector.tensor_scalar(weight[:], coef[:], inv_total[:], None, ALU.mult)
+        nc.vector.tensor_scalar(ws_first[:], mixed[:], inv_total[:], None, ALU.mult)
 
-        for c0 in range(0, T, N_STORE):
-            cols = slice(c0, c0 + N_STORE)
-            y = sb.tile([P, N_STORE], F32, name=f"y{c0}")
+        nc.vector.tensor_copy(wf[:].indirect(offsets(offs_sb, first)), ws_first[:])
+        own_rest = sb.tile([P, n_rest], F32, name="own_rest")
+        run_rest = sb.tile([P, n_rest], F32, name="run_rest")
+        nc.scalar.activation(own_rest[:], p[:, rest], ACT.Copy, scale=weight[:, 0:1])
+        nc.scalar.activation(by_runs(run_rest[:]), spread(run_sum_rest[:], n_rest), ACT.Copy, scale=weight[:, 1:2])
+        nc.vector.tensor_tensor(wf[:].indirect(offsets(offs_sb, rest)), own_rest[:], run_rest[:], ALU.add)
+
+        c0 = 0
+        for k, width in enumerate(STORE_WIDTHS):
+            cols = slice(c0, c0 + width)
+            y = sb.tile([P, width], F32, name=f"y{k}")
             nc.vector.scalar_tensor_tensor(y[:], old_sb[:, cols], fade_sb[:], wf[:, cols], ALU.mult, ALU.add)
-            nc.sync.dma_start(out=out[:, cols], in_=y[:])
+            queue = nc.sync if k % 2 == 0 else nc.scalar
+            queue.dma_start(out=out[:, cols], in_=y[:])
+            c0 += width

@@ -19,27 +19,40 @@ AX = mybir.AxisListType
 
 P = 128
 PACK = 4
-N_MM = 256
+KEY_HALF = T // 2
 HALF = SLOTS // 2
-EXP_CAP = 2.0 ** 60
+LINEAR_FROM = 43.0
 SQRT_E = math.sqrt(math.e)
-N_DIVIDE = 96
+N_DIVIDED = 160
 N_FIRST = 160
-STORE_WIDTHS = (256,256,256,256)
+STORE_WIDTHS = (320, 320, 256, 128)
 
 
-def offsets(tile, slots):
-    return tile[:, slots.start // 16 : slots.stop // 16]
+def runs_of(widths):
+    starts = [sum(widths[:k]) for k in range(len(widths))]
+    return [slice(c0, c0 + w) for c0, w in zip(starts, widths)]
 
 
-def quantize_queries(nc, pool, raw, tag):
+def offsets(list_tile, slots):
+    return list_tile[:, slots.start // 16 : slots.stop // 16]
+
+
+def interleaved(ap, pattern):
+    return ap.rearrange(pattern + " -> p c t i", i=4)
+
+
+def quantize_queries(nc, pool, raw, tag, scalar_columns):
     grouped = pool.tile([P, Q, PACK], BF16, name=tag + "_grouped", align_bytes=64)
-    codes = pool.tile([P, Q], U32, name=tag + "_codes", align_bytes=64)
+    codes = pool.tile([P, Q], U32, name=tag + "_codes", tag=tag + "_codes", align_bytes=64)
     scales = pool.tile([P, Q], U8, name=tag + "_scales", align_bytes=64)
+    split = Q - scalar_columns
     nc.vector.tensor_copy(
-        out=grouped[:].rearrange("p (c i) t -> p c t i", i=4),
-        in_=raw[:].rearrange("p t (c i) -> p c t i", i=4),
+        interleaved(grouped[:, 0:split, :], "p (c i) t"), interleaved(raw[:, :, 0:split], "p t (c i)")
     )
+    if scalar_columns:
+        nc.scalar.activation(
+            interleaved(grouped[:, split:Q, :], "p (c i) t"), interleaved(raw[:, :, split:Q], "p t (c i)"), ACT.Copy
+        )
     nc.vector.quantize_mx(
         out=codes[:].bitcast(FP8X4), scales=scales[:], in_=grouped[:].rearrange("p w t -> p (w t)")
     )
@@ -58,20 +71,20 @@ def tile_attend_worthfor_smoothpage_counts_heads_kernel(
         offs2_sb = sb.tile([P, SLOTS // 16], U16, name="offs2_sb")
         key_scales = sb.tile([P, T], U8, name="key_scales", align_bytes=64)
         nc.vector.memset(key_scales[:].bitcast(I32), 0)
+
+        q2_raw = sb.tile([P, PACK, Q], F32, name="q2_raw")
+        q_raw = sb.tile([P, PACK, Q], F32, name="q_raw")
+        key_codes = [sb.tile([P, KEY_HALF], U32, name=f"key_codes{h}", align_bytes=64) for h in range(2)]
+        words = keys_words[0].rearrange("p n t -> p (n t)").bitcast(I32)
         scale_words = keys_scales[0].bitcast(I32)
+        nc.sync.dma_start(out=q2_raw[:], in_=query2.rearrange("(p t) w -> p t w", t=PACK))
+        nc.sync.dma_start(out=key_codes[0][:].bitcast(I32), in_=words[:, 0:KEY_HALF])
         for quad in range(4):
-            nc.scalar.dma_start(
+            nc.sync.dma_start(
                 out=key_scales[32 * quad : 32 * quad + 4, :].bitcast(I32),
                 in_=scale_words[4 * quad : 4 * quad + 4, :],
             )
-
-        q2_raw = sb.tile([P, PACK, Q], F32, name="q2_raw")
-        nc.sync.dma_start(out=q2_raw[:], in_=query2.rearrange("(p t) w -> p t w", t=PACK))
-        words = keys_words[0].rearrange("p n t -> p (n t)").bitcast(I32)
-        key_codes = [sb.tile([P, T // 2], U32, name=f"key_codes{h}", align_bytes=64) for h in range(2)]
-        for h in range(2):
-            nc.sync.dma_start(out=key_codes[h][:].bitcast(I32), in_=words[:, h * T // 2 : (h + 1) * T // 2])
-        q_raw = sb.tile([P, PACK, Q], F32, name="q_raw")
+        nc.sync.dma_start(out=key_codes[1][:].bitcast(I32), in_=words[:, KEY_HALF:T])
         nc.sync.dma_start(out=q_raw[:], in_=query.rearrange("(p t) w -> p t w", t=PACK))
         nc.sync.dma_start(offs2_sb[:], offs2)
         nc.sync.dma_start(offs_sb[:], offs)
@@ -85,97 +98,99 @@ def tile_attend_worthfor_smoothpage_counts_heads_kernel(
         nc.sync.dma_start(out=old_sb[:], in_=old)
 
         one = sb.tile([P, 1], F32, name="one")
+        half = sb.tile([P, 1], F32, name="half")
         sqrt_e = sb.tile([P, 1], F32, name="sqrt_e")
         wf = sb.tile([P, T], F32, name="wf")
         nc.vector.memset(one[:], 1.0)
+        nc.vector.memset(half[:], 0.5)
         nc.scalar.activation(sqrt_e[:], one[:], ACT.Copy, scale=SQRT_E)
         nc.vector.memset(wf[:], 0.0)
-        coef = sb.tile([P, 2], F32, name="coef")
-        nc.gpsimd.tensor_scalar(coef[:, 0:1], mix_sb[:], -256.0, 256.0, ALU.mult, ALU.add)
-        nc.gpsimd.tensor_scalar(coef[:, 1:2], mix_sb[:], 256.0 / RUN, 0.0, ALU.mult, ALU.add)
 
-        def scores(codes, scales, tag, widths, on_scalar):
-            whole = sb.tile([P, T], F32, name=tag)
-            c0 = 0
-            for n, width in enumerate(widths):
-                cols = slice(c0, c0 + width)
-                h, k0 = divmod(c0, T // 2)
-                acc = psum.tile([P, width], F32, name=f"{tag}_acc{n}")
+        def scores(codes, scales, tag, widths, banks, on_vector):
+            whole = sb.tile([P, T], F32, name=tag, tag=tag)
+            for n, cols in enumerate(runs_of(widths)):
+                h, k0 = divmod(cols.start, KEY_HALF)
+                acc = psum.tile([P, widths[n]], F32, name=f"{tag}_acc{n}", tag=f"bank{banks[n]}")
                 nc.tensor.matmul_mx(
                     out=acc[:],
                     lhsT=codes[:].bitcast(FP8X4),
                     lhsT_scale=scales[:],
-                    rhs=key_codes[h][:, k0 : k0 + width].bitcast(FP8X4),
+                    rhs=key_codes[h][:, k0 : k0 + widths[n]].bitcast(FP8X4),
                     rhs_scale=key_scales[:, cols],
                     start=True,
                     stop=True,
                 )
-                if n < on_scalar:
-                    nc.scalar.activation(whole[:, cols], acc[:], ACT.Copy)
-                else:
+                if n in on_vector:
                     nc.vector.tensor_copy(whole[:, cols], acc[:])
-                c0 += width
+                else:
+                    nc.scalar.activation(whole[:, cols], acc[:], ACT.Copy)
             return whole
 
         low, high = slice(0, HALF), slice(HALF, SLOTS)
+        divided = slice(0, N_DIVIDED)
+        logged = [slice(HALF, HALF + HALF // 2), slice(HALF + HALF // 2, SLOTS), slice(N_DIVIDED, HALF)]
 
-        q2_codes, q2_scales = quantize_queries(nc, sb, q2_raw, "q2")
-        q_codes, q_scales = quantize_queries(nc, sb, q_raw, "q")
-        b_all = scores(q2_codes, q2_scales, "b_all", (256, 256, 256, 128, 128), 3)
+        q2_codes, q2_scales = quantize_queries(nc, sb, q2_raw, "q2", 48)
+        b_all = scores(q2_codes, q2_scales, "b_all", (256, 256, 256, 256), (0, 1, 2, 3), (0,))
+        q_codes, q_scales = quantize_queries(nc, sb, q_raw, "q", 0)
 
         b_sel = sb.tile([P, SLOTS], F32, name="b_sel")
         e = sb.tile([P, SLOTS], F32, name="e")
-        e_cap = sb.tile([P, SLOTS], F32, name="e_cap")
         nc.scalar.activation(e[:, high], b_all[:].indirect(offsets(offs2_sb, high)), ACT.Exp)
         nc.vector.tensor_copy(b_sel[:, low], b_all[:].indirect(offsets(offs2_sb, low)))
         nc.scalar.activation(e[:, low], b_sel[:, low], ACT.Exp)
-
         nc.vector.tensor_copy(b_sel[:, high], b_all[:].indirect(offsets(offs2_sb, high)))
-        nc.vector.tensor_scalar(e_cap[:], e[:], EXP_CAP, None, ALU.min)
 
-        a_all = scores(q_codes, q_scales, "a_all", (512, 512), 0)
+        a_all = scores(q_codes, q_scales, "a_all", (256, 256, 512), (3, 2, 1), (1, 2))
+        b_plus_half = sb.tile([P, N_DIVIDED], F32, name="b_plus_half")
+        nc.vector.tensor_scalar(b_plus_half[:], b_sel[:, divided], 0.5, None, ALU.add)
         a_sel = sb.tile([P, SLOTS], F32, name="a_sel")
-        nc.vector.tensor_copy(a_sel[:, high], a_all[:].indirect(offsets(offs_sb, high)))
+        nc.vector.tensor_copy(a_sel[:], a_all[:].indirect(offs_sb[:]))
 
-        n_logged = SLOTS - N_DIVIDE
-        divided = slice(n_logged, SLOTS)
-        logged = [slice(n_logged * k // 3, n_logged * (k + 1) // 3) for k in range(3)]
-        capped_den = sb.tile([P, SLOTS], F32, name="capped_den")
-        den = sb.tile([P, SLOTS], F32, name="den")
-        log_den = sb.tile([P, SLOTS], F32, name="log_den")
-        inv_den = sb.tile([P, SLOTS], F32, name="inv_den")
-        for part in logged + [divided]:
-            nc.scalar.activation(capped_den[:, part], e_cap[:, part], ACT.Ln, bias=sqrt_e[:], scale=SQRT_E)
-            nc.vector.scalar_tensor_tensor(den[:, part], b_sel[:, part], 0.5, capped_den[:, part], ALU.add, ALU.max)
+        log1p = sb.tile([P, SLOTS], F32, name="log1p", tag="q_codes", align_bytes=64)
+        soft = sb.tile([P, SLOTS], F32, name="soft", tag="a_all")
+        log_den = sb.tile([P, SLOTS], F32, name="log_den", tag="log_then_coef")
         for part in logged:
-            nc.scalar.activation(log_den[:, part], den[:, part], ACT.Ln)
+            nc.scalar.activation(log1p[:, part], e[:, part], ACT.Ln, bias=one[:])
+            nc.vector.scalar_tensor_tensor(soft[:, part], log1p[:, part], LINEAR_FROM, b_sel[:, part], ALU.min, ALU.max)
+        nc.scalar.activation(log1p[:, divided], e[:, divided], ACT.Ln, bias=sqrt_e[:], scale=SQRT_E)
+        nc.vector.scalar_tensor_tensor(soft[:, divided], log1p[:, divided], LINEAR_FROM + 0.5, b_plus_half[:], ALU.min, ALU.max)
+        for part in logged:
+            nc.scalar.activation(log_den[:, part], soft[:, part], ACT.Ln, bias=half[:])
 
-        nc.vector.tensor_copy(a_sel[:, low], a_all[:].indirect(offsets(offs_sb, low)))
-        nc.vector.reciprocal(inv_den[:, divided], den[:, divided])
-        s_tile = sb.tile([P, 1 + SLOTS], F32, name="s_tile")
-        s = s_tile[:, 1:]
+        inv_divided = sb.tile([P, N_DIVIDED], F32, name="inv_divided", tag="inv_then_s")
+        nc.vector.reciprocal(inv_divided[:], soft[:, divided])
+        inv_logged = sb.tile([P, SLOTS], F32, name="inv_logged")
 
-        def slot_scores(part):
-            nc.vector.scalar_tensor_tensor(s[:, part], a_sel[:, part], lam_sb[:], inv_den[:, part], ALU.mult, ALU.mult)
-
-        slot_scores(divided)
-        nc.vector.tensor_reduce(s_tile[:, 0:1], s[:, divided], AX.X, ALU.max)
-        for part in (low, slice(HALF, n_logged)):
-            nc.scalar.activation(inv_den[:, part], log_den[:, part], ACT.Exp, scale=-1.0)
-            slot_scores(part)
+        s_first = sb.tile([P, N_DIVIDED], F32, name="s_first")
+        nc.vector.scalar_tensor_tensor(s_first[:], a_sel[:, divided], lam_sb[:], inv_divided[:], ALU.mult, ALU.mult)
+        n_rest = SLOTS - N_DIVIDED
+        s_rest = sb.tile([P, n_rest + 1], F32, name="s_rest", tag="inv_then_s")
+        nc.vector.tensor_reduce(s_rest[:, n_rest : n_rest + 1], s_first[:], AX.X, ALU.max)
+        for part in logged:
+            nc.scalar.activation(inv_logged[:, part], log_den[:, part], ACT.Exp, scale=-1.0)
+            nc.vector.scalar_tensor_tensor(
+                s_rest[:, part.start - N_DIVIDED : part.stop - N_DIVIDED],
+                a_sel[:, part],
+                lam_sb[:],
+                inv_logged[:, part],
+                ALU.mult,
+                ALU.mult,
+            )
         neg_max = sb.tile([P, 1], F32, name="neg_max")
-        nc.vector.tensor_reduce(neg_max[:], s_tile[:, 0 : 1 + n_logged], AX.X, ALU.max, negate=True)
+        nc.vector.tensor_reduce(neg_max[:], s_rest[:], AX.X, ALU.max, negate=True)
+
+        coef = sb.tile([P, 2], F32, name="coef", tag="log_then_coef")
+        nc.scalar.activation(coef[:, 0:1], mix_sb[:], ACT.Copy, scale=-256.0, bias=256.0)
+        nc.scalar.activation(coef[:, 1:2], mix_sb[:], ACT.Copy, scale=256.0 / RUN)
 
         first, rest = slice(0, N_FIRST), slice(N_FIRST, SLOTS)
-        n_rest = SLOTS - N_FIRST
         p = sb.tile([P, SLOTS], F32, name="p")
+        total = sb.tile([P, 1], F32, name="total")
         part_sum = sb.tile([P, 2], F32, name="part_sum")
-        run_sum_first = sb.tile([P, N_FIRST // RUN], F32, name="run_sum_first")
-        run_sum_rest = sb.tile([P, n_rest // RUN], F32, name="run_sum_rest")
-        for k, part in enumerate((first, rest)):
-            nc.scalar.activation(
-                p[:, part], s[:, part], ACT.Exp, bias=neg_max[:], accum_out=part_sum[:, k : k + 1]
-            )
+        for k, (part, s) in enumerate(((first, s_first[:]), (rest, s_rest[:, 0:n_rest]))):
+            nc.scalar.activation(p[:, part], s, ACT.Exp, bias=neg_max[:], accum_out=part_sum[:, k : k + 1])
+        p_first = p[:, first]
 
         def by_runs(ap):
             return ap.rearrange("p (g r) -> p g r", r=RUN)
@@ -183,14 +198,15 @@ def tile_attend_worthfor_smoothpage_counts_heads_kernel(
         def spread(ap, n):
             return ap.unsqueeze(2).to_broadcast([P, n // RUN, RUN])
 
+        run_sum_first = sb.tile([P, N_FIRST // RUN], F32, name="run_sum_first")
+        run_sum_rest = sb.tile([P, n_rest // RUN], F32, name="run_sum_rest")
         run_part = sb.tile([P, N_FIRST // RUN], F32, name="run_part")
         mixed = sb.tile([P, N_FIRST], F32, name="mixed")
-        nc.vector.tensor_reduce(run_sum_first[:], by_runs(p[:, first]), AX.X, ALU.add)
+        nc.vector.tensor_reduce(run_sum_first[:], by_runs(p_first[:]), AX.X, ALU.add)
         nc.vector.tensor_scalar(run_part[:], run_sum_first[:], coef[:, 1:2], None, ALU.mult)
         nc.vector.scalar_tensor_tensor(
-            by_runs(mixed[:]), by_runs(p[:, first]), coef[:, 0:1], spread(run_part[:], N_FIRST), ALU.mult, ALU.add
+            by_runs(mixed[:]), by_runs(p_first[:]), coef[:, 0:1], spread(run_part[:], N_FIRST), ALU.mult, ALU.add
         )
-        total = sb.tile([P, 1], F32, name="total")
         inv_total = sb.tile([P, 1], F32, name="inv_total")
         weight = sb.tile([P, 2], F32, name="weight")
         ws_first = sb.tile([P, N_FIRST], F32, name="ws_first")
@@ -199,7 +215,6 @@ def tile_attend_worthfor_smoothpage_counts_heads_kernel(
         nc.vector.reciprocal(inv_total[:], total[:])
         nc.vector.tensor_scalar(weight[:], coef[:], inv_total[:], None, ALU.mult)
         nc.vector.tensor_scalar(ws_first[:], mixed[:], inv_total[:], None, ALU.mult)
-
         nc.vector.tensor_copy(wf[:].indirect(offsets(offs_sb, first)), ws_first[:])
         own_rest = sb.tile([P, n_rest], F32, name="own_rest")
         run_rest = sb.tile([P, n_rest], F32, name="run_rest")
@@ -207,11 +222,8 @@ def tile_attend_worthfor_smoothpage_counts_heads_kernel(
         nc.scalar.activation(by_runs(run_rest[:]), spread(run_sum_rest[:], n_rest), ACT.Copy, scale=weight[:, 1:2])
         nc.vector.tensor_tensor(wf[:].indirect(offsets(offs_sb, rest)), own_rest[:], run_rest[:], ALU.add)
 
-        c0 = 0
-        for k, width in enumerate(STORE_WIDTHS):
-            cols = slice(c0, c0 + width)
-            y = sb.tile([P, width], F32, name=f"y{k}")
+        for k, cols in enumerate(runs_of(STORE_WIDTHS)):
+            y = sb.tile([P, STORE_WIDTHS[k]], F32, name=f"y{k}")
             nc.vector.scalar_tensor_tensor(y[:], old_sb[:, cols], fade_sb[:], wf[:, cols], ALU.mult, ALU.add)
             queue = nc.sync if k % 2 == 0 else nc.scalar
             queue.dma_start(out=out[:, cols], in_=y[:])
-            c0 += width

@@ -160,7 +160,7 @@ def tile_attend_worthfor_smoothpage_counts_heads_kernel(
 
         inv_divided = sb.tile([P, N_DIVIDED], F32, name="inv_divided", tag="inv_then_s")
         nc.vector.reciprocal(inv_divided[:], soft[:, divided])
-        inv_logged = sb.tile([P, SLOTS], F32, name="inv_logged")
+        inv_logged = sb.tile([P, SLOTS], F32, name="inv_logged", tag="inv_then_p")
 
         s_first = sb.tile([P, N_DIVIDED], F32, name="s_first")
         nc.vector.scalar_tensor_tensor(s_first[:], a_sel[:, divided], lam_sb[:], inv_divided[:], ALU.mult, ALU.mult)
@@ -185,12 +185,18 @@ def tile_attend_worthfor_smoothpage_counts_heads_kernel(
         nc.scalar.activation(coef[:, 1:2], mix_sb[:], ACT.Copy, scale=256.0 / RUN)
 
         first, rest = slice(0, N_FIRST), slice(N_FIRST, SLOTS)
-        p = sb.tile([P, SLOTS], F32, name="p")
+        first_max = s_rest[:, n_rest : n_rest + 1]
+        neg_first_max = sb.tile([P, 1], F32, name="neg_first_max")
+        p_first = sb.tile([P, N_FIRST], F32, name="p_first", tag="inv_then_p")
+        p_rest = sb.tile([P, n_rest], F32, name="p_rest")
+        sum_first = sb.tile([P, 1], F32, name="sum_first")
+        sum_rest = sb.tile([P, 1], F32, name="sum_rest")
+        shift = sb.tile([P, 1], F32, name="shift")
         total = sb.tile([P, 1], F32, name="total")
-        part_sum = sb.tile([P, 2], F32, name="part_sum")
-        for k, (part, s) in enumerate(((first, s_first[:]), (rest, s_rest[:, 0:n_rest]))):
-            nc.scalar.activation(p[:, part], s, ACT.Exp, bias=neg_max[:], accum_out=part_sum[:, k : k + 1])
-        p_first = p[:, first]
+        nc.scalar.activation(neg_first_max[:], first_max, ACT.Copy, scale=-1.0)
+        nc.scalar.activation(p_first[:], s_first[:], ACT.Exp, bias=neg_first_max[:], accum_out=sum_first[:])
+        nc.scalar.activation(shift[:], first_max, ACT.Exp, bias=neg_max[:])
+        nc.scalar.activation(p_rest[:], s_rest[:, 0:n_rest], ACT.Exp, bias=neg_max[:], accum_out=sum_rest[:])
 
         def by_runs(ap):
             return ap.rearrange("p (g r) -> p g r", r=RUN)
@@ -210,15 +216,18 @@ def tile_attend_worthfor_smoothpage_counts_heads_kernel(
         inv_total = sb.tile([P, 1], F32, name="inv_total")
         weight = sb.tile([P, 2], F32, name="weight")
         ws_first = sb.tile([P, N_FIRST], F32, name="ws_first")
-        nc.vector.tensor_tensor(total[:], part_sum[:, 0:1], part_sum[:, 1:2], ALU.add)
-        nc.vector.tensor_reduce(run_sum_rest[:], by_runs(p[:, rest]), AX.X, ALU.add)
+        nc.vector.scalar_tensor_tensor(total[:], sum_first[:], shift[:], sum_rest[:], ALU.mult, ALU.add)
         nc.vector.reciprocal(inv_total[:], total[:])
+        nc.vector.tensor_scalar(ws_first[:], mixed[:], inv_total[:], shift[:], ALU.mult, ALU.mult)
         nc.vector.tensor_scalar(weight[:], coef[:], inv_total[:], None, ALU.mult)
-        nc.vector.tensor_scalar(ws_first[:], mixed[:], inv_total[:], None, ALU.mult)
+        for part in (slice(0, n_rest // 2), slice(n_rest // 2, n_rest)):
+            nc.vector.tensor_reduce(
+                run_sum_rest[:, part.start // RUN : part.stop // RUN], by_runs(p_rest[:, part]), AX.X, ALU.add
+            )
         nc.vector.tensor_copy(wf[:].indirect(offsets(offs_sb, first)), ws_first[:])
         own_rest = sb.tile([P, n_rest], F32, name="own_rest")
         run_rest = sb.tile([P, n_rest], F32, name="run_rest")
-        nc.scalar.activation(own_rest[:], p[:, rest], ACT.Copy, scale=weight[:, 0:1])
+        nc.scalar.activation(own_rest[:], p_rest[:], ACT.Copy, scale=weight[:, 0:1])
         nc.scalar.activation(by_runs(run_rest[:]), spread(run_sum_rest[:], n_rest), ACT.Copy, scale=weight[:, 1:2])
         nc.vector.tensor_tensor(wf[:].indirect(offsets(offs_sb, rest)), own_rest[:], run_rest[:], ALU.add)
 

@@ -23,8 +23,8 @@ KEY_HALF = T // 2
 HALF = SLOTS // 2
 LINEAR_FROM = 43.0
 SQRT_E = math.sqrt(math.e)
-N_DIVIDED = 160
-N_FIRST = 160
+N_DIVIDED = 192
+N_FIRST = 192
 STORE_WIDTHS = (320, 320, 256, 128)
 
 

import math
from contextlib import ExitStack

import concourse.mybir as mybir

D, T, SLOTS, Q, RUN = 512, 1024, 512, 128, 8
FLOPS = 2 * 2 * D * Q * T

F32 = mybir.dt.float32
BF16 = mybir.dt.bfloat16
I32 = mybir.dt.int32
U32 = mybir.dt.uint32
U16 = mybir.dt.uint16
U8 = mybir.dt.uint8
FP8X4 = mybir.dt.float8_e4m3fn_x4
ALU = mybir.AluOpType
ACT = mybir.ActivationFunctionType
AX = mybir.AxisListType

P = 128
PACK = 4
KEY_HALF = T // 2
HALF = SLOTS // 2
LINEAR_FROM = 43.0
SQRT_E = math.sqrt(math.e)
N_DIVIDED = 192
N_FIRST = 192
STORE_WIDTHS = (320, 320, 256, 128)


def runs_of(widths):
    starts = [sum(widths[:k]) for k in range(len(widths))]
    return [slice(c0, c0 + w) for c0, w in zip(starts, widths)]


def offsets(list_tile, slots):
    return list_tile[:, slots.start // 16 : slots.stop // 16]


def interleaved(ap, pattern):
    return ap.rearrange(pattern + " -> p c t i", i=4)


def quantize_queries(nc, pool, raw, tag, scalar_columns):
    grouped = pool.tile([P, Q, PACK], BF16, name=tag + "_grouped", align_bytes=64)
    codes = pool.tile([P, Q], U32, name=tag + "_codes", tag=tag + "_codes", align_bytes=64)
    scales = pool.tile([P, Q], U8, name=tag + "_scales", align_bytes=64)
    split = Q - scalar_columns
    nc.vector.tensor_copy(
        interleaved(grouped[:, 0:split, :], "p (c i) t"), interleaved(raw[:, :, 0:split], "p t (c i)")
    )
    if scalar_columns:
        nc.scalar.activation(
            interleaved(grouped[:, split:Q, :], "p (c i) t"), interleaved(raw[:, :, split:Q], "p t (c i)"), ACT.Copy
        )
    nc.vector.quantize_mx(
        out=codes[:].bitcast(FP8X4), scales=scales[:], in_=grouped[:].rearrange("p w t -> p (w t)")
    )
    return codes, scales


def tile_attend_worthfor_smoothpage_counts_heads_kernel(
    tc, query, query2, keys_words, keys_scales, lam, mix, old, fade, offs, offs2, out
):
    nc = tc.nc
    with ExitStack() as ctx:
        sb = ctx.enter_context(tc.tile_pool(name="sb", bufs=1))
        psum = ctx.enter_context(tc.psum_pool(name="psum", bufs=1))

        offs_sb = sb.tile([P, SLOTS // 16], U16, name="offs_sb")
        offs2_sb = sb.tile([P, SLOTS // 16], U16, name="offs2_sb")
        key_scales = sb.tile([P, T], U8, name="key_scales", align_bytes=64)
        nc.vector.memset(key_scales[:].bitcast(I32), 0)

        q2_raw = sb.tile([P, PACK, Q], F32, name="q2_raw")
        q_raw = sb.tile([P, PACK, Q], F32, name="q_raw")
        key_codes = [sb.tile([P, KEY_HALF], U32, name=f"key_codes{h}", align_bytes=64) for h in range(2)]
        words = keys_words[0].rearrange("p n t -> p (n t)").bitcast(I32)
        scale_words = keys_scales[0].bitcast(I32)
        nc.sync.dma_start(out=q2_raw[:], in_=query2.rearrange("(p t) w -> p t w", t=PACK))
        nc.sync.dma_start(out=key_codes[0][:].bitcast(I32), in_=words[:, 0:KEY_HALF])
        for quad in range(4):
            nc.sync.dma_start(
                out=key_scales[32 * quad : 32 * quad + 4, :].bitcast(I32),
                in_=scale_words[4 * quad : 4 * quad + 4, :],
            )
        nc.sync.dma_start(out=key_codes[1][:].bitcast(I32), in_=words[:, KEY_HALF:T])
        nc.sync.dma_start(out=q_raw[:], in_=query.rearrange("(p t) w -> p t w", t=PACK))
        nc.sync.dma_start(offs2_sb[:], offs2)
        nc.sync.dma_start(offs_sb[:], offs)
        lam_sb = sb.tile([P, 1], F32, name="lam_sb")
        mix_sb = sb.tile([P, 1], F32, name="mix_sb")
        fade_sb = sb.tile([P, 1], F32, name="fade_sb")
        old_sb = sb.tile([P, T], F32, name="old_sb")
        nc.sync.dma_start(out=lam_sb[:], in_=lam)
        nc.sync.dma_start(out=mix_sb[:], in_=mix)
        nc.sync.dma_start(out=fade_sb[:], in_=fade)
        nc.sync.dma_start(out=old_sb[:], in_=old)

        one = sb.tile([P, 1], F32, name="one")
        half = sb.tile([P, 1], F32, name="half")
        sqrt_e = sb.tile([P, 1], F32, name="sqrt_e")
        wf = sb.tile([P, T], F32, name="wf")
        nc.vector.memset(one[:], 1.0)
        nc.vector.memset(half[:], 0.5)
        nc.scalar.activation(sqrt_e[:], one[:], ACT.Copy, scale=SQRT_E)
        nc.vector.memset(wf[:], 0.0)

        def scores(codes, scales, tag, widths, banks, on_vector):
            whole = sb.tile([P, T], F32, name=tag, tag=tag)
            for n, cols in enumerate(runs_of(widths)):
                h, k0 = divmod(cols.start, KEY_HALF)
                acc = psum.tile([P, widths[n]], F32, name=f"{tag}_acc{n}", tag=f"bank{banks[n]}")
                nc.tensor.matmul_mx(
                    out=acc[:],
                    lhsT=codes[:].bitcast(FP8X4),
                    lhsT_scale=scales[:],
                    rhs=key_codes[h][:, k0 : k0 + widths[n]].bitcast(FP8X4),
                    rhs_scale=key_scales[:, cols],
                    start=True,
                    stop=True,
                )
                if n in on_vector:
                    nc.vector.tensor_copy(whole[:, cols], acc[:])
                else:
                    nc.scalar.activation(whole[:, cols], acc[:], ACT.Copy)
            return whole

        low, high = slice(0, HALF), slice(HALF, SLOTS)
        divided = slice(0, N_DIVIDED)
        logged = [slice(HALF, HALF + HALF // 2), slice(HALF + HALF // 2, SLOTS), slice(N_DIVIDED, HALF)]

        q2_codes, q2_scales = quantize_queries(nc, sb, q2_raw, "q2", 48)
        b_all = scores(q2_codes, q2_scales, "b_all", (256, 256, 256, 256), (0, 1, 2, 3), (0,))
        q_codes, q_scales = quantize_queries(nc, sb, q_raw, "q", 0)

        b_sel = sb.tile([P, SLOTS], F32, name="b_sel")
        e = sb.tile([P, SLOTS], F32, name="e")
        nc.scalar.activation(e[:, high], b_all[:].indirect(offsets(offs2_sb, high)), ACT.Exp)
        nc.vector.tensor_copy(b_sel[:, low], b_all[:].indirect(offsets(offs2_sb, low)))
        nc.scalar.activation(e[:, low], b_sel[:, low], ACT.Exp)
        nc.vector.tensor_copy(b_sel[:, high], b_all[:].indirect(offsets(offs2_sb, high)))

        a_all = scores(q_codes, q_scales, "a_all", (256, 256, 512), (3, 2, 1), (1, 2))
        b_plus_half = sb.tile([P, N_DIVIDED], F32, name="b_plus_half")
        nc.vector.tensor_scalar(b_plus_half[:], b_sel[:, divided], 0.5, None, ALU.add)
        a_sel = sb.tile([P, SLOTS], F32, name="a_sel")
        nc.vector.tensor_copy(a_sel[:], a_all[:].indirect(offs_sb[:]))

        log1p = sb.tile([P, SLOTS], F32, name="log1p", tag="q_codes", align_bytes=64)
        soft = sb.tile([P, SLOTS], F32, name="soft", tag="a_all")
        log_den = sb.tile([P, SLOTS], F32, name="log_den", tag="log_then_coef")
        for part in logged:
            nc.scalar.activation(log1p[:, part], e[:, part], ACT.Ln, bias=one[:])
            nc.vector.scalar_tensor_tensor(soft[:, part], log1p[:, part], LINEAR_FROM, b_sel[:, part], ALU.min, ALU.max)
        nc.scalar.activation(log1p[:, divided], e[:, divided], ACT.Ln, bias=sqrt_e[:], scale=SQRT_E)
        nc.vector.scalar_tensor_tensor(soft[:, divided], log1p[:, divided], LINEAR_FROM + 0.5, b_plus_half[:], ALU.min, ALU.max)
        for part in logged:
            nc.scalar.activation(log_den[:, part], soft[:, part], ACT.Ln, bias=half[:])

        inv_divided = sb.tile([P, N_DIVIDED], F32, name="inv_divided", tag="inv_then_s")
        nc.vector.reciprocal(inv_divided[:], soft[:, divided])
        inv_logged = sb.tile([P, SLOTS], F32, name="inv_logged", tag="inv_then_p")

        s_first = sb.tile([P, N_DIVIDED], F32, name="s_first")
        nc.vector.scalar_tensor_tensor(s_first[:], a_sel[:, divided], lam_sb[:], inv_divided[:], ALU.mult, ALU.mult)
        n_rest = SLOTS - N_DIVIDED
        s_rest = sb.tile([P, n_rest + 1], F32, name="s_rest", tag="inv_then_s")
        nc.vector.tensor_reduce(s_rest[:, n_rest : n_rest + 1], s_first[:], AX.X, ALU.max)
        for part in logged:
            nc.scalar.activation(inv_logged[:, part], log_den[:, part], ACT.Exp, scale=-1.0)
            nc.vector.scalar_tensor_tensor(
                s_rest[:, part.start - N_DIVIDED : part.stop - N_DIVIDED],
                a_sel[:, part],
                lam_sb[:],
                inv_logged[:, part],
                ALU.mult,
                ALU.mult,
            )
        neg_max = sb.tile([P, 1], F32, name="neg_max")
        nc.vector.tensor_reduce(neg_max[:], s_rest[:], AX.X, ALU.max, negate=True)

        coef = sb.tile([P, 2], F32, name="coef", tag="log_then_coef")
        nc.scalar.activation(coef[:, 0:1], mix_sb[:], ACT.Copy, scale=-256.0, bias=256.0)
        nc.scalar.activation(coef[:, 1:2], mix_sb[:], ACT.Copy, scale=256.0 / RUN)

        first, rest = slice(0, N_FIRST), slice(N_FIRST, SLOTS)
        first_max = s_rest[:, n_rest : n_rest + 1]
        neg_first_max = sb.tile([P, 1], F32, name="neg_first_max")
        p_first = sb.tile([P, N_FIRST], F32, name="p_first", tag="inv_then_p")
        p_rest = sb.tile([P, n_rest], F32, name="p_rest")
        sum_first = sb.tile([P, 1], F32, name="sum_first")
        sum_rest = sb.tile([P, 1], F32, name="sum_rest")
        shift = sb.tile([P, 1], F32, name="shift")
        total = sb.tile([P, 1], F32, name="total")
        nc.scalar.activation(neg_first_max[:], first_max, ACT.Copy, scale=-1.0)
        nc.scalar.activation(p_first[:], s_first[:], ACT.Exp, bias=neg_first_max[:], accum_out=sum_first[:])
        nc.scalar.activation(shift[:], first_max, ACT.Exp, bias=neg_max[:])
        nc.scalar.activation(p_rest[:], s_rest[:, 0:n_rest], ACT.Exp, bias=neg_max[:], accum_out=sum_rest[:])

        def by_runs(ap):
            return ap.rearrange("p (g r) -> p g r", r=RUN)

        def spread(ap, n):
            return ap.unsqueeze(2).to_broadcast([P, n // RUN, RUN])

        run_sum_first = sb.tile([P, N_FIRST // RUN], F32, name="run_sum_first")
        run_sum_rest = sb.tile([P, n_rest // RUN], F32, name="run_sum_rest")
        run_part = sb.tile([P, N_FIRST // RUN], F32, name="run_part")
        mixed = sb.tile([P, N_FIRST], F32, name="mixed")
        nc.vector.tensor_reduce(run_sum_first[:], by_runs(p_first[:]), AX.X, ALU.add)
        nc.vector.tensor_scalar(run_part[:], run_sum_first[:], coef[:, 1:2], None, ALU.mult)
        nc.vector.scalar_tensor_tensor(
            by_runs(mixed[:]), by_runs(p_first[:]), coef[:, 0:1], spread(run_part[:], N_FIRST), ALU.mult, ALU.add
        )
        inv_total = sb.tile([P, 1], F32, name="inv_total")
        weight = sb.tile([P, 2], F32, name="weight")
        ws_first = sb.tile([P, N_FIRST], F32, name="ws_first")
        nc.vector.scalar_tensor_tensor(total[:], sum_first[:], shift[:], sum_rest[:], ALU.mult, ALU.add)
        nc.vector.reciprocal(inv_total[:], total[:])
        nc.vector.tensor_scalar(ws_first[:], mixed[:], inv_total[:], shift[:], ALU.mult, ALU.mult)
        nc.vector.tensor_scalar(weight[:], coef[:], inv_total[:], None, ALU.mult)
        for part in (slice(0, n_rest // 2), slice(n_rest // 2, n_rest)):
            nc.vector.tensor_reduce(
                run_sum_rest[:, part.start // RUN : part.stop // RUN], by_runs(p_rest[:, part]), AX.X, ALU.add
            )
        nc.vector.tensor_copy(wf[:].indirect(offsets(offs_sb, first)), ws_first[:])
        own_rest = sb.tile([P, n_rest], F32, name="own_rest")
        run_rest = sb.tile([P, n_rest], F32, name="run_rest")
        nc.scalar.activation(own_rest[:], p_rest[:], ACT.Copy, scale=weight[:, 0:1])
        nc.scalar.activation(by_runs(run_rest[:]), spread(run_sum_rest[:], n_rest), ACT.Copy, scale=weight[:, 1:2])
        nc.vector.tensor_tensor(wf[:].indirect(offsets(offs_sb, rest)), own_rest[:], run_rest[:], ALU.add)

        for k, cols in enumerate(runs_of(STORE_WIDTHS)):
            y = sb.tile([P, STORE_WIDTHS[k]], F32, name=f"y{k}")
            nc.vector.scalar_tensor_tensor(y[:], old_sb[:, cols], fade_sb[:], wf[:, cols], ALU.mult, ALU.add)
            queue = nc.sync if k % 2 == 0 else nc.scalar
            queue.dma_start(out=out[:, cols], in_=y[:])
